import numpy as np
import ml_dtypes


def mxq(x, axis, fmt="e4m3"):
    dtype, down = {"e4m3": (ml_dtypes.float8_e4m3fn, 7), "e5m2": (ml_dtypes.float8_e5m2, 14)}[fmt]
    v = np.moveaxis(np.asarray(x, np.float32).astype(ml_dtypes.bfloat16).astype(np.float64), axis, -1)
    blocks = v.reshape(v.shape[:-1] + (-1, 32))
    amax = np.abs(blocks).max(-1, keepdims=True)
    byte = np.maximum(np.where(amax > 0, np.frexp(amax)[1] - 1 + 127, 0) - down, 1)
    scale = np.exp2(byte - 127.0)
    codes = (blocks / scale).astype(np.float32).astype(dtype).astype(np.float64)
    return np.moveaxis((codes * scale).reshape(v.shape), -1, axis)


WIDE = False


def mx_kscale(k):
    if not WIDE:
        return np.ones(k)
    levels = np.array([10, -10, 5, -5, 0])
    if k % 512:
        return np.exp2(np.random.permutation(np.resize(levels, k // 32))).repeat(32)
    a = np.empty((k // 512, 16))
    for p in range(k // 512):
        a[p, :8] = np.random.permutation(np.resize(levels, 8))
        for g in range(8):
            far = levels[np.abs(levels - a[p, g]) >= 10]
            a[p, g + 8] = far[np.random.randint(len(far))]
    return np.exp2(a.ravel()).repeat(32)


def f64(x):
    return np.asarray(x).astype(np.float64)


def striped(idx):
    return np.tile(idx.reshape(-1, 16).T, (8, 1)).astype(np.uint16)


def unstriped(offs):
    return offs[:16].T.reshape(-1).astype(np.int64)


def pack_weight(w):
    k, n = w.shape
    w = f64(np.asarray(w, np.float32).astype(ml_dtypes.bfloat16)).reshape(k // 32, 32, n)
    amax = np.abs(w).max(1)
    byte = np.clip(np.where(amax > 0, np.frexp(amax)[1] - 1 + 127 - 7, 1), 1, 254)
    scaled = (w * np.exp2(127.0 - byte)[:, None, :]).reshape(k, n).astype(np.float32)
    words = np.ascontiguousarray(scaled.reshape(k // 512, 128, 4, n).transpose(0, 1, 3, 2)).astype(ml_dtypes.float8_e4m3fn).view(np.uint8)
    return words, np.ascontiguousarray(byte.astype(np.uint8).reshape(k // 512, 16, n))


def unpack_weight(words, scales):
    g, p, n, _ = words.shape
    vals = np.ascontiguousarray(words).view(ml_dtypes.float8_e4m3fn).astype(np.float64) * np.repeat(np.exp2(scales.astype(np.float64) - 127.0), 8, axis=1)[..., None]
    return vals.transpose(0, 1, 3, 2).reshape(g * 512, n)


def sigmoid(v):
    return 1.0 / (1.0 + np.exp(-np.maximum(v, -700.0)))

def planes(y):
    n, m = y.shape
    v = y.astype(np.float32).astype(ml_dtypes.bfloat16).astype(np.float64).reshape(n // 32, 32, m)
    top = np.abs(v).max(1)
    byte = np.clip(np.where(top > 0, np.frexp(top)[1] - 1 + 127 - 7, 1), 1, 254)
    codes = (v * np.exp2(127.0 - byte)[:, None, :]).reshape(n, m).astype(np.float32).astype(ml_dtypes.float8_e4m3fn).view(np.uint8)
    words = codes.reshape(n // 512, 128, 4, m).transpose(0, 1, 3, 2)
    return np.ascontiguousarray(words), np.ascontiguousarray(byte.astype(np.uint8).reshape(n // 512, 16, m))


K, T, S, V, N = 512, 1024, 512, 256, 512


def setup_inputs():
    n = np.random.standard_normal
    s = mx_kscale(K)[:, None]
    packed_xT = pack_weight(n((K, T)) * s)
    return {
        "x_words": packed_xT[0],
        "x_scales": packed_xT[1],
        "w1": (n((K, N)) / np.sqrt(K) / s).astype(np.float32),
        "offs": striped(np.random.permutation(T)[:S]),
        "win": striped(np.random.permutation(S)[:V]),
        "lose": striped(np.random.permutation(S)[:V]),
    }


def reference(x_words, x_scales, w1, offs, win, lose):
    xq = unpack_weight(x_words, x_scales)[:, unstriped(offs)]
    y = mxq(f64(w1), 0, "e4m3").T @ xq
    out_0 = sigmoid(y[:, unstriped(win)] - y[:, unstriped(lose)])
    return (out_0,) + planes(out_0)

@@ -1,0 +1,177 @@
+from contextlib import ExitStack
+
+import concourse.mybir as mybir
+
+K, T, S, V, N = 512, 1024, 512, 256, 512
+P = 128
+PACK = 4
+FLOPS = 2 * K * S * N
+
+F32 = mybir.dt.float32
+BF16 = mybir.dt.bfloat16
+I32 = mybir.dt.int32
+U32 = mybir.dt.uint32
+U16 = mybir.dt.uint16
+U8 = mybir.dt.uint8
+FP8X4 = mybir.dt.float8_e4m3fn_x4
+ACT = mybir.ActivationFunctionType
+ALU = mybir.AluOpType
+
+
+def tile_picked_ranknet_sigmoid_po_kernel(tc, x_words, x_scales, w1, offs, win, lose, out_0, out_1, out_2):
+    nc = tc.nc
+    with ExitStack() as ctx:
+        lists = ctx.enter_context(tc.tile_pool(name="lists", bufs=1))
+        sb = ctx.enter_context(tc.tile_pool(name="sb", bufs=1))
+        ps = ctx.enter_context(tc.psum_pool(name="ps", bufs=1))
+
+        offs_t = lists.tile([P, S // 16], U16, name="offs_t")
+        win_t = lists.tile([P, V // 16], U16, name="win_t")
+        lose_t = lists.tile([P, V // 16], U16, name="lose_t")
+
+        xs_all = sb.tile([P, T], U8, name="xs_all", align_bytes=64)
+        xw_all = sb.tile([P, T], I32, name="xw_all", align_bytes=64)
+        HALF = N // 2
+        w_rows = w1.rearrange("(p j) c -> p j c", j=PACK)
+        w_raw = [sb.tile([P, PACK, HALF], F32, name=f"w_raw{h}") for h in range(2)]
+        nc.vector.memset(xs_all[:].bitcast(I32), 0)
+        nc.sync.dma_start(offs_t[:], offs)
+        nc.sync.dma_start(xw_all[:], x_words[0].rearrange("p c r -> p (c r)").bitcast(I32))
+        for q in range(4):
+            nc.sync.dma_start(xs_all[32 * q : 32 * q + 4, :].bitcast(I32), x_scales[0, 4 * q : 4 * q + 4, :].bitcast(I32))
+        for h in range(2):
+            nc.sync.dma_start(w_raw[h][:], w_rows[:, :, h * HALF : (h + 1) * HALF])
+        nc.sync.dma_start(win_t[:], win)
+        nc.sync.dma_start(lose_t[:], lose)
+
+        warm_in = sb.tile([P, 1], F32, name="warm_in")
+        warm_out = sb.tile([P, 1], F32, name="warm_out")
+        nc.gpsimd.memset(warm_in[:], 0.0)
+        nc.scalar.activation(warm_out[:], warm_in[:], ACT.Sigmoid)
+
+        xs = sb.tile([P, S], U8, name="xs", align_bytes=64)
+        xw = sb.tile([P, S], I32, name="xw", align_bytes=64)
+        w_bf = sb.tile([P, PACK, P, PACK], BF16, name="w_bf", align_bytes=64)
+        w_codes = [sb.tile([P, P], U32, name=f"w_codes{t}", align_bytes=64) for t in range(PACK)]
+        w_scales = [sb.tile([P, P], U8, name=f"w_scales{t}", align_bytes=64) for t in range(PACK)]
+        HS = S // 2
+        banks = [[ps.tile([P, HS], F32, name=f"bank{t}_{u}") for u in range(2)] for t in range(PACK)]
+
+        def deal(engine_copy, h, c0, c1):
+            m0 = (h * HALF + c0) // PACK
+            m1 = (h * HALF + c1) // PACK
+            engine_copy(
+                w_bf[:, :, m0:m1, :].rearrange("p t (a i) j -> p a j i t", i=2),
+                w_raw[h][:, :, c0:c1].rearrange("p j (a i t) -> p a j i t", i=2, t=PACK),
+            )
+
+        def gather_words(a, b):
+            nc.vector.tensor_copy(xw[:, a:b].bitcast(U32), xw_all[:].bitcast(U32).indirect(offs_t[:, a // 16 : b // 16]))
+
+        def gather_bytes(a, b):
+            nc.vector.tensor_copy(xs[:, a:b], xs_all[:].indirect(offs_t[:, a // 16 : b // 16]))
+
+        def quant_w(t, m0, m1):
+            nc.vector.quantize_mx(
+                out=w_codes[t][:, m0:m1].bitcast(FP8X4),
+                scales=w_scales[t][:, m0:m1],
+                in_=w_bf[:, t, m0:m1, :].rearrange("p m j -> p (m j)"),
+            )
+
+        def product(t, u):
+            cols = slice(u * HS, (u + 1) * HS)
+            nc.tensor.matmul_mx(
+                out=banks[t][u][:],
+                lhsT=w_codes[t][:].bitcast(FP8X4),
+                lhsT_scale=w_scales[t][:],
+                rhs=xw[:, cols].bitcast(FP8X4),
+                rhs_scale=xs[:, cols],
+                start=True,
+                stop=True,
+            )
+
+        y = [sb.tile([P, S], F32, name=f"y{t}") for t in range(PACK)]
+        loser = [sb.tile([P, V], F32, name=f"loser{t}") for t in range(PACK)]
+        diff = [sb.tile([P, V], F32, name=f"diff{t}") for t in range(PACK)]
+        prob = sb.tile([P, PACK, V], F32, name="prob")
+        out_rows = out_0.rearrange("(p t) v -> p t v", t=PACK)
+        prob_bf = sb.tile([P, V, PACK], BF16, name="prob_bf", align_bytes=64)
+        o_codes = sb.tile([P, V], U32, name="o_codes", align_bytes=64)
+        o_scales = sb.tile([P, V], U8, name="o_scales", align_bytes=64)
+
+        def evac(copy, t, u):
+            copy(y[t][:, u * HS : (u + 1) * HS], banks[t][u][:])
+
+        def lose_scalar(t, a, b):
+            nc.scalar.activation(loser[t][:, a:b], y[t][:].indirect(lose_t[:, a // 16 : b // 16]), ACT.Copy)
+
+        def lose_vector(t, a, b):
+            nc.vector.tensor_copy(loser[t][:, a:b], y[t][:].indirect(lose_t[:, a // 16 : b // 16]))
+
+        def difference(t, a, b):
+            nc.vector.tensor_tensor(diff[t][:, a:b], y[t][:].indirect(win_t[:, a // 16 : b // 16]), loser[t][:, a:b], ALU.subtract)
+
+        def sigmoid(t, a, b):
+            nc.scalar.activation(prob[:, t, a:b], diff[t][:, a:b], ACT.Sigmoid)
+
+        def store_rows(t0, t1):
+            nc.sync.dma_start(out_rows[:, t0:t1, :], prob[:, t0:t1, :])
+
+        def weave(copy, a, b):
+            copy(
+                prob_bf[:, a:b, :].rearrange("p (c i) t -> p c t i", i=4),
+                prob[:, :, a:b].rearrange("p t (c i) -> p c t i", i=4),
+            )
+
+        def quant_out(a, b):
+            nc.vector.quantize_mx(
+                out=o_codes[:, a:b].bitcast(FP8X4),
+                scales=o_scales[:, a:b],
+                in_=prob_bf[:, a:b, :].rearrange("p c t -> p (c t)"),
+            )
+
+        def store_words(queue, a, b):
+            queue.dma_start(out_1[0, :, a:b, :].rearrange("p c r -> p (c r)").bitcast(I32), o_codes[:, a:b].bitcast(I32))
+
+        def store_scales(queue, q):
+            queue.dma_start(out_2[0, 4 * q : 4 * q + 4, :].bitcast(I32), o_scales[32 * q : 32 * q + 4, :].bitcast(I32))
+
+        gather_words(0, S)
+        gather_bytes(0, S)
+        deal(nc.scalar.copy, 0, 0, HALF)
+        deal(nc.vector.tensor_copy, 1, 0, 176)
+        deal(nc.scalar.copy, 1, 176, HALF)
+        for t in range(PACK):
+            quant_w(t, 0, P)
+            product(t, 0)
+            product(t, 1)
+        evac(nc.scalar.copy, 0, 0)
+        evac(nc.vector.tensor_copy, 0, 1)
+        evac(nc.scalar.copy, 1, 0)
+        evac(nc.scalar.copy, 1, 1)
+        lose_scalar(1, 0, V)
+        evac(nc.vector.tensor_copy, 2, 0)
+        evac(nc.scalar.copy, 2, 1)
+        evac(nc.vector.tensor_copy, 3, 0)
+        evac(nc.vector.tensor_copy, 3, 1)
+        lose_vector(0, 0, V)
+        lose_scalar(2, 0, V)
+        lose_scalar(3, 0, V)
+        for t in range(PACK - 1):
+            difference(t, 0, V)
+        difference(3, 0, 128)
+        difference(3, 128, V)
+        for t in range(PACK - 1):
+            sigmoid(t, 0, V)
+            if t > 0:
+                store_rows(0 if t == 1 else t, t + 1)
+        sigmoid(3, 0, 128)
+        sigmoid(3, 128, V)
+        store_rows(3, 4)
+        weave(nc.vector.tensor_copy, 0, 128)
+        weave(nc.vector.tensor_copy, 128, 192)
+        weave(nc.scalar.copy, 192, V)
+        quant_out(0, V)
+        store_words(nc.sync, 0, V)
+        for q in range(4):
+            store_scales(nc.scalar if q < 2 else nc.sync, q)

@@ -33,14 +33,14 @@ def tile_picked_ranknet_sigmoid_po_kernel(tc, x_words, x_scales, w1, offs, win, 
         xw_all = sb.tile([P, T], I32, name="xw_all", align_bytes=64)
         HALF = N // 2
         w_rows = w1.rearrange("(p j) c -> p j c", j=PACK)
-        w_raw = [sb.tile([P, PACK, HALF], F32, name=f"w_raw{h}") for h in range(2)]
+        w_raw = [sb.tile([P, 2, N], F32, name=f"w_raw{h}") for h in range(2)]
         nc.vector.memset(xs_all[:].bitcast(I32), 0)
         nc.sync.dma_start(offs_t[:], offs)
         nc.sync.dma_start(xw_all[:], x_words[0].rearrange("p c r -> p (c r)").bitcast(I32))
-        for q in range(4):
-            nc.sync.dma_start(xs_all[32 * q : 32 * q + 4, :].bitcast(I32), x_scales[0, 4 * q : 4 * q + 4, :].bitcast(I32))
+        for r in range(4):
+            nc.sync.dma_start(xs_all[r:P:32, :].bitcast(I32), x_scales[0, r:16:4, :].bitcast(I32))
         for h in range(2):
-            nc.sync.dma_start(w_raw[h][:], w_rows[:, :, h * HALF : (h + 1) * HALF])
+            nc.sync.dma_start(w_raw[h][:], w_rows[:, 2 * h : 2 * h + 2, :])
         nc.sync.dma_start(win_t[:], win)
         nc.sync.dma_start(lose_t[:], lose)
 
@@ -57,13 +57,6 @@ def tile_picked_ranknet_sigmoid_po_kernel(tc, x_words, x_scales, w1, offs, win, 
         HS = S // 2
         banks = [[ps.tile([P, HS], F32, name=f"bank{t}_{u}") for u in range(2)] for t in range(PACK)]
 
-        def deal(engine_copy, h, c0, c1):
-            m0 = (h * HALF + c0) // PACK
-            m1 = (h * HALF + c1) // PACK
-            engine_copy(
-                w_bf[:, :, m0:m1, :].rearrange("p t (a i) j -> p a j i t", i=2),
-                w_raw[h][:, :, c0:c1].rearrange("p j (a i t) -> p a j i t", i=2, t=PACK),
-            )
 
         def gather_words(a, b):
             nc.vector.tensor_copy(xw[:, a:b].bitcast(U32), xw_all[:].bitcast(U32).indirect(offs_t[:, a // 16 : b // 16]))
@@ -136,11 +129,18 @@ def tile_picked_ranknet_sigmoid_po_kernel(tc, x_words, x_scales, w1, offs, win, 
         def store_scales(queue, q):
             queue.dma_start(out_2[0, 4 * q : 4 * q + 4, :].bitcast(I32), o_scales[32 * q : 32 * q + 4, :].bitcast(I32))
 
+        def deal_pair(engine_copy, h, t0):
+            engine_copy(
+                w_bf[:, t0 : t0 + 2, :, 2 * h : 2 * h + 2].rearrange("p t (a i) j -> p a j i t", i=4),
+                w_raw[h][:].rearrange("p j (a i t) -> p a j i t", i=4, t=PACK)[:, :, :, :, t0 : t0 + 2],
+            )
+
         gather_words(0, S)
         gather_bytes(0, S)
-        deal(nc.scalar.copy, 0, 0, HALF)
-        deal(nc.vector.tensor_copy, 1, 0, 176)
-        deal(nc.scalar.copy, 1, 176, HALF)
+        deal_pair(nc.scalar.copy, 0, 0)
+        deal_pair(nc.scalar.copy, 0, 2)
+        deal_pair(nc.vector.tensor_copy, 1, 0)
+        deal_pair(nc.scalar.copy, 1, 2)
         for t in range(PACK):
             quant_w(t, 0, P)
             product(t, 0)
@@ -148,30 +148,34 @@ def tile_picked_ranknet_sigmoid_po_kernel(tc, x_words, x_scales, w1, offs, win, 
         evac(nc.scalar.copy, 0, 0)
         evac(nc.vector.tensor_copy, 0, 1)
         evac(nc.scalar.copy, 1, 0)
-        evac(nc.scalar.copy, 1, 1)
-        lose_scalar(1, 0, V)
+        evac(nc.vector.tensor_copy, 1, 1)
+        lose_scalar(0, 0, V)
         evac(nc.vector.tensor_copy, 2, 0)
+        lose_vector(1, 0, V)
         evac(nc.scalar.copy, 2, 1)
-        evac(nc.vector.tensor_copy, 3, 0)
-        evac(nc.vector.tensor_copy, 3, 1)
-        lose_vector(0, 0, V)
+        evac(nc.scalar.copy, 3, 0)
+        evac(nc.scalar.copy, 3, 1)
         lose_scalar(2, 0, V)
         lose_scalar(3, 0, V)
         for t in range(PACK - 1):
             difference(t, 0, V)
         difference(3, 0, 128)
-        difference(3, 128, V)
+        difference(3, 128, 192)
+        difference(3, 192, V)
         for t in range(PACK - 1):
             sigmoid(t, 0, V)
-            if t > 0:
-                store_rows(0 if t == 1 else t, t + 1)
+            if t == 1:
+                store_rows(0, 2)
         sigmoid(3, 0, 128)
-        sigmoid(3, 128, V)
-        store_rows(3, 4)
+        sigmoid(3, 128, 192)
+        sigmoid(3, 192, V)
+        store_rows(2, 4)
         weave(nc.vector.tensor_copy, 0, 128)
         weave(nc.vector.tensor_copy, 128, 192)
-        weave(nc.scalar.copy, 192, V)
-        quant_out(0, V)
-        store_words(nc.sync, 0, V)
+        quant_out(0, 128)
+        weave(nc.vector.tensor_copy, 192, V)
+        store_words(nc.sync, 0, 128)
+        quant_out(128, V)
+        store_words(nc.sync, 128, V)
         for q in range(4):
             store_scales(nc.scalar if q < 2 else nc.sync, q)

@@ -33,14 +33,14 @@ def tile_picked_ranknet_sigmoid_po_kernel(tc, x_words, x_scales, w1, offs, win, 
         xw_all = sb.tile([P, T], I32, name="xw_all", align_bytes=64)
         HALF = N // 2
         w_rows = w1.rearrange("(p j) c -> p j c", j=PACK)
-        w_raw = [sb.tile([P, 2, N], F32, name=f"w_raw{h}") for h in range(2)]
+        w_raw = [sb.tile([P, PACK, HALF], F32, name=f"w_raw{h}") for h in range(2)]
         nc.vector.memset(xs_all[:].bitcast(I32), 0)
-        nc.sync.dma_start(offs_t[:], offs)
         nc.sync.dma_start(xw_all[:], x_words[0].rearrange("p c r -> p (c r)").bitcast(I32))
+        nc.sync.dma_start(offs_t[:], offs)
         for r in range(4):
             nc.sync.dma_start(xs_all[r:P:32, :].bitcast(I32), x_scales[0, r:16:4, :].bitcast(I32))
         for h in range(2):
-            nc.sync.dma_start(w_raw[h][:], w_rows[:, 2 * h : 2 * h + 2, :])
+            nc.sync.dma_start(w_raw[h][:], w_rows[:, :, h * HALF : (h + 1) * HALF])
         nc.sync.dma_start(win_t[:], win)
         nc.sync.dma_start(lose_t[:], lose)
 
@@ -129,18 +129,19 @@ def tile_picked_ranknet_sigmoid_po_kernel(tc, x_words, x_scales, w1, offs, win, 
         def store_scales(queue, q):
             queue.dma_start(out_2[0, 4 * q : 4 * q + 4, :].bitcast(I32), o_scales[32 * q : 32 * q + 4, :].bitcast(I32))
 
-        def deal_pair(engine_copy, h, t0):
+        def deal_pair(engine_copy, h, t0, m0, m1):
             engine_copy(
-                w_bf[:, t0 : t0 + 2, :, 2 * h : 2 * h + 2].rearrange("p t (a i) j -> p a j i t", i=4),
-                w_raw[h][:].rearrange("p j (a i t) -> p a j i t", i=4, t=PACK)[:, :, :, :, t0 : t0 + 2],
+                w_bf[:, t0 : t0 + 2, h * 64 + m0 : h * 64 + m1, :].rearrange("p t (a i) j -> p a j i t", i=4),
+                w_raw[h][:, :, PACK * m0 : PACK * m1].rearrange("p j (a i t) -> p a j i t", i=4, t=PACK)[:, :, :, :, t0 : t0 + 2],
             )
 
         gather_words(0, S)
         gather_bytes(0, S)
-        deal_pair(nc.scalar.copy, 0, 0)
-        deal_pair(nc.scalar.copy, 0, 2)
-        deal_pair(nc.vector.tensor_copy, 1, 0)
-        deal_pair(nc.scalar.copy, 1, 2)
+        deal_pair(nc.scalar.copy, 0, 0, 0, 64)
+        deal_pair(nc.scalar.copy, 0, 2, 0, 64)
+        deal_pair(nc.vector.tensor_copy, 1, 0, 0, 48)
+        deal_pair(nc.scalar.copy, 1, 0, 48, 64)
+        deal_pair(nc.scalar.copy, 1, 2, 0, 64)
         for t in range(PACK):
             quant_w(t, 0, P)
             product(t, 0)

from contextlib import ExitStack

import concourse.mybir as mybir

K, T, S, V, N = 512, 1024, 512, 256, 512
P = 128
PACK = 4
FLOPS = 2 * K * S * N

F32 = mybir.dt.float32
BF16 = mybir.dt.bfloat16
I32 = mybir.dt.int32
U32 = mybir.dt.uint32
U16 = mybir.dt.uint16
U8 = mybir.dt.uint8
FP8X4 = mybir.dt.float8_e4m3fn_x4
ACT = mybir.ActivationFunctionType
ALU = mybir.AluOpType


def tile_picked_ranknet_sigmoid_po_kernel(tc, x_words, x_scales, w1, offs, win, lose, out_0, out_1, out_2):
    nc = tc.nc
    with ExitStack() as ctx:
        lists = ctx.enter_context(tc.tile_pool(name="lists", bufs=1))
        sb = ctx.enter_context(tc.tile_pool(name="sb", bufs=1))
        ps = ctx.enter_context(tc.psum_pool(name="ps", bufs=1))

        offs_t = lists.tile([P, S // 16], U16, name="offs_t")
        win_t = lists.tile([P, V // 16], U16, name="win_t")
        lose_t = lists.tile([P, V // 16], U16, name="lose_t")

        xs_all = sb.tile([P, T], U8, name="xs_all", align_bytes=64)
        xw_all = sb.tile([P, T], I32, name="xw_all", align_bytes=64)
        HALF = N // 2
        w_rows = w1.rearrange("(p j) c -> p j c", j=PACK)
        w_raw = [sb.tile([P, PACK, HALF], F32, name=f"w_raw{h}") for h in range(2)]
        nc.vector.memset(xs_all[:].bitcast(I32), 0)
        nc.sync.dma_start(xw_all[:], x_words[0].rearrange("p c r -> p (c r)").bitcast(I32))
        nc.sync.dma_start(offs_t[:], offs)
        for r in range(4):
            nc.sync.dma_start(xs_all[r:P:32, :].bitcast(I32), x_scales[0, r:16:4, :].bitcast(I32))
        for h in range(2):
            nc.sync.dma_start(w_raw[h][:], w_rows[:, :, h * HALF : (h + 1) * HALF])
        nc.sync.dma_start(win_t[:], win)
        nc.sync.dma_start(lose_t[:], lose)

        warm_in = sb.tile([P, 1], F32, name="warm_in")
        warm_out = sb.tile([P, 1], F32, name="warm_out")
        nc.gpsimd.memset(warm_in[:], 0.0)
        nc.scalar.activation(warm_out[:], warm_in[:], ACT.Sigmoid)

        xs = sb.tile([P, S], U8, name="xs", align_bytes=64)
        xw = sb.tile([P, S], I32, name="xw", align_bytes=64)
        w_bf = sb.tile([P, PACK, P, PACK], BF16, name="w_bf", align_bytes=64)
        w_codes = [sb.tile([P, P], U32, name=f"w_codes{t}", align_bytes=64) for t in range(PACK)]
        w_scales = [sb.tile([P, P], U8, name=f"w_scales{t}", align_bytes=64) for t in range(PACK)]
        HS = S // 2
        banks = [[ps.tile([P, HS], F32, name=f"bank{t}_{u}") for u in range(2)] for t in range(PACK)]


        def gather_words(a, b):
            nc.vector.tensor_copy(xw[:, a:b].bitcast(U32), xw_all[:].bitcast(U32).indirect(offs_t[:, a // 16 : b // 16]))

        def gather_bytes(a, b):
            nc.vector.tensor_copy(xs[:, a:b], xs_all[:].indirect(offs_t[:, a // 16 : b // 16]))

        def quant_w(t, m0, m1):
            nc.vector.quantize_mx(
                out=w_codes[t][:, m0:m1].bitcast(FP8X4),
                scales=w_scales[t][:, m0:m1],
                in_=w_bf[:, t, m0:m1, :].rearrange("p m j -> p (m j)"),
            )

        def product(t, u):
            cols = slice(u * HS, (u + 1) * HS)
            nc.tensor.matmul_mx(
                out=banks[t][u][:],
                lhsT=w_codes[t][:].bitcast(FP8X4),
                lhsT_scale=w_scales[t][:],
                rhs=xw[:, cols].bitcast(FP8X4),
                rhs_scale=xs[:, cols],
                start=True,
                stop=True,
            )

        y = [sb.tile([P, S], F32, name=f"y{t}") for t in range(PACK)]
        loser = [sb.tile([P, V], F32, name=f"loser{t}") for t in range(PACK)]
        diff = [sb.tile([P, V], F32, name=f"diff{t}") for t in range(PACK)]
        prob = sb.tile([P, PACK, V], F32, name="prob")
        out_rows = out_0.rearrange("(p t) v -> p t v", t=PACK)
        prob_bf = sb.tile([P, V, PACK], BF16, name="prob_bf", align_bytes=64)
        o_codes = sb.tile([P, V], U32, name="o_codes", align_bytes=64)
        o_scales = sb.tile([P, V], U8, name="o_scales", align_bytes=64)

        def evac(copy, t, u):
            copy(y[t][:, u * HS : (u + 1) * HS], banks[t][u][:])

        def lose_scalar(t, a, b):
            nc.scalar.activation(loser[t][:, a:b], y[t][:].indirect(lose_t[:, a // 16 : b // 16]), ACT.Copy)

        def lose_vector(t, a, b):
            nc.vector.tensor_copy(loser[t][:, a:b], y[t][:].indirect(lose_t[:, a // 16 : b // 16]))

        def difference(t, a, b):
            nc.vector.tensor_tensor(diff[t][:, a:b], y[t][:].indirect(win_t[:, a // 16 : b // 16]), loser[t][:, a:b], ALU.subtract)

        def sigmoid(t, a, b):
            nc.scalar.activation(prob[:, t, a:b], diff[t][:, a:b], ACT.Sigmoid)

        def store_rows(t0, t1):
            nc.sync.dma_start(out_rows[:, t0:t1, :], prob[:, t0:t1, :])

        def weave(copy, a, b):
            copy(
                prob_bf[:, a:b, :].rearrange("p (c i) t -> p c t i", i=4),
                prob[:, :, a:b].rearrange("p t (c i) -> p c t i", i=4),
            )

        def quant_out(a, b):
            nc.vector.quantize_mx(
                out=o_codes[:, a:b].bitcast(FP8X4),
                scales=o_scales[:, a:b],
                in_=prob_bf[:, a:b, :].rearrange("p c t -> p (c t)"),
            )

        def store_words(queue, a, b):
            queue.dma_start(out_1[0, :, a:b, :].rearrange("p c r -> p (c r)").bitcast(I32), o_codes[:, a:b].bitcast(I32))

        def store_scales(queue, q):
            queue.dma_start(out_2[0, 4 * q : 4 * q + 4, :].bitcast(I32), o_scales[32 * q : 32 * q + 4, :].bitcast(I32))

        def deal_pair(engine_copy, h, t0, m0, m1):
            engine_copy(
                w_bf[:, t0 : t0 + 2, h * 64 + m0 : h * 64 + m1, :].rearrange("p t (a i) j -> p a j i t", i=4),
                w_raw[h][:, :, PACK * m0 : PACK * m1].rearrange("p j (a i t) -> p a j i t", i=4, t=PACK)[:, :, :, :, t0 : t0 + 2],
            )

        gather_words(0, S)
        gather_bytes(0, S)
        deal_pair(nc.scalar.copy, 0, 0, 0, 64)
        deal_pair(nc.scalar.copy, 0, 2, 0, 64)
        deal_pair(nc.vector.tensor_copy, 1, 0, 0, 48)
        deal_pair(nc.scalar.copy, 1, 0, 48, 64)
        deal_pair(nc.scalar.copy, 1, 2, 0, 64)
        for t in range(PACK):
            quant_w(t, 0, P)
            product(t, 0)
            product(t, 1)
        evac(nc.scalar.copy, 0, 0)
        evac(nc.vector.tensor_copy, 0, 1)
        evac(nc.scalar.copy, 1, 0)
        evac(nc.vector.tensor_copy, 1, 1)
        lose_scalar(0, 0, V)
        evac(nc.vector.tensor_copy, 2, 0)
        lose_vector(1, 0, V)
        evac(nc.scalar.copy, 2, 1)
        evac(nc.scalar.copy, 3, 0)
        evac(nc.scalar.copy, 3, 1)
        lose_scalar(2, 0, V)
        lose_scalar(3, 0, V)
        for t in range(PACK - 1):
            difference(t, 0, V)
        difference(3, 0, 128)
        difference(3, 128, 192)
        difference(3, 192, V)
        for t in range(PACK - 1):
            sigmoid(t, 0, V)
            if t == 1:
                store_rows(0, 2)
        sigmoid(3, 0, 128)
        sigmoid(3, 128, 192)
        sigmoid(3, 192, V)
        store_rows(2, 4)
        weave(nc.vector.tensor_copy, 0, 128)
        weave(nc.vector.tensor_copy, 128, 192)
        quant_out(0, 128)
        weave(nc.vector.tensor_copy, 192, V)
        store_words(nc.sync, 0, 128)
        quant_out(128, V)
        store_words(nc.sync, 128, V)
        for q in range(4):
            store_scales(nc.scalar if q < 2 else nc.sync, q)
